import numpy as np
import ml_dtypes


def mxq(x, axis, fmt="e4m3"):
    dtype, down = {"e4m3": (ml_dtypes.float8_e4m3fn, 7), "e5m2": (ml_dtypes.float8_e5m2, 14)}[fmt]
    v = np.moveaxis(np.asarray(x, np.float32).astype(ml_dtypes.bfloat16).astype(np.float64), axis, -1)
    blocks = v.reshape(v.shape[:-1] + (-1, 32))
    amax = np.abs(blocks).max(-1, keepdims=True)
    byte = np.maximum(np.where(amax > 0, np.frexp(amax)[1] - 1 + 127, 0) - down, 1)
    scale = np.exp2(byte - 127.0)
    codes = (blocks / scale).astype(np.float32).astype(dtype).astype(np.float64)
    return np.moveaxis((codes * scale).reshape(v.shape), -1, axis)


WIDE = False


def mx_kscale(k):
    if not WIDE:
        return np.ones(k)
    levels = np.array([10, -10, 5, -5, 0])
    if k % 512:
        return np.exp2(np.random.permutation(np.resize(levels, k // 32))).repeat(32)
    a = np.empty((k // 512, 16))
    for p in range(k // 512):
        a[p, :8] = np.random.permutation(np.resize(levels, 8))
        for g in range(8):
            far = levels[np.abs(levels - a[p, g]) >= 10]
            a[p, g + 8] = far[np.random.randint(len(far))]
    return np.exp2(a.ravel()).repeat(32)


def f64(x):
    return np.asarray(x).astype(np.float64)


def striped(idx):
    return np.tile(np.asarray(idx).reshape(-1, 16).T, (8, 1)).astype(np.uint16)


def unstriped(offs):
    return offs[:16].T.reshape(-1).astype(np.int64)


E2M1 = np.array([0.0, 0.5, 1.0, 1.5, 2.0, 3.0, 4.0, 6.0, -0.0, -0.5, -1.0, -1.5, -2.0, -3.0, -4.0, -6.0])


def pack_weight(w, fmt):
    k, n = w.shape
    w = f64(np.asarray(w, np.float32).astype(ml_dtypes.bfloat16)).reshape(k // 32, 32, n)
    amax = np.abs(w).max(1)
    if fmt == "e4m3":
        byte = np.frexp(amax)[1] - 1 + 127 - 7
    else:
        mant, ex = np.frexp(amax / 6.0)
        byte = np.where(mant > 0.5, ex, ex - 1) + 127
    byte = np.clip(np.where(amax > 0, byte, 1), 1, 254)
    scaled = (w * np.exp2(127.0 - byte)[:, None, :]).reshape(k, n).astype(np.float32)
    by_word = np.ascontiguousarray(scaled.reshape(k // 512, 128, 4, n).transpose(0, 1, 3, 2))
    if fmt == "e4m3":
        words = by_word.astype(ml_dtypes.float8_e4m3fn).view(np.uint8)
    else:
        c = by_word.astype(ml_dtypes.float4_e2m1fn).view(np.uint8) & 0xF
        words = (c[..., 0::2] | (c[..., 1::2] << 4)).reshape(k // 512, 128, 2 * n)
    return np.ascontiguousarray(words), np.ascontiguousarray(byte.astype(np.uint8).reshape(k // 512, 16, n))


def unpack_weight(words, scales, fmt):
    g, _, n = scales.shape
    words = np.ascontiguousarray(words).reshape(g, 128, n, -1)
    if fmt == "e4m3":
        vals = words.view(ml_dtypes.float8_e4m3fn).astype(np.float64)
    else:
        nib = np.empty((g, 128, n, 4), np.uint8)
        nib[..., 0::2] = words & 0xF
        nib[..., 1::2] = words >> 4
        vals = E2M1[nib]
    vals = vals * np.repeat(np.exp2(scales.astype(np.float64) - 127.0), 8, axis=1)[..., None]
    return vals.transpose(0, 1, 3, 2).reshape(g * 512, n)


D, K, T, I, Q, E = 512, 1024, 1024, 256, 128, 512


def setup_inputs():
    n = np.random.standard_normal
    idx = np.random.permutation(T)[:I]
    fd = mx_kscale(D)
    fk = mx_kscale(K)
    ft = mx_kscale(T)
    fkeysp = pack_weight(n((K, T)) / fk[:, None], "e4m3")
    return {
        "query": (n((D, Q)) * 0.25 / np.sqrt(D) * fd[:, None]).astype(np.float32),
        "fquery": (n((K, Q)) * 0.5 / np.sqrt(K) * fk[:, None]).astype(np.float32),
        "ckeys": (n((D, T)) / fd[:, None]).astype(np.float32),
        "fkeys_words": fkeysp[0],
        "fkeys_scales": fkeysp[1],
        "fac": (np.random.uniform(0.5, 2.0, (1, T)) * ft).astype(np.float32),
        "vals": (n((T, E)) / ft[:, None]).astype(np.float32),
        "offs": striped(idx),
    }


def reference(query, fquery, ckeys, fkeys_words, fkeys_scales, fac, vals, offs):
    idx = unstriped(offs)
    fkeysu = unpack_weight(fkeys_words, fkeys_scales, "e4m3")
    queryq = mxq(f64(query), 0, "e4m3")
    ckeysq = mxq(f64(ckeys), 0, "e4m3")
    a = queryq.T @ ckeysq
    fqueryq = mxq(f64(fquery), 0, "e4m3")
    fkeysidxg = fkeysu[:, idx]
    b = fqueryq.T @ fkeysidxg
    dl = b - a[:, idx]
    df = np.zeros((Q, T))
    df[:, idx] = dl
    s = a + df
    p = np.exp(s - np.max(s, axis=1, keepdims=True))
    w = p * f64(fac) / np.sum(p, axis=1, keepdims=True)
    wt = w.T
    wtq = mxq(wt, 0, "e4m3")
    valsq = mxq(f64(vals), 0, "e4m3")
    o = wtq.T @ valsq
    return o

@@ -1,0 +1,209 @@
+from contextlib import ExitStack
+
+import concourse.mybir as mybir
+from concourse.masks import make_identity
+
+D, K, T, I, Q, E = 512, 1024, 1024, 256, 128, 512
+FLOPS = 2 * Q * (D * T + K * I + T * E)
+
+F32 = mybir.dt.float32
+BF16 = mybir.dt.bfloat16
+I32 = mybir.dt.int32
+U32 = mybir.dt.uint32
+U16 = mybir.dt.uint16
+U8 = mybir.dt.uint8
+FP8X4 = mybir.dt.float8_e4m3fn_x4
+ALU = mybir.AluOpType
+ACT = mybir.ActivationFunctionType
+AX = mybir.AxisListType
+
+P = 128
+PACK = 4
+PASS = P * PACK
+BANK = 512
+CHUNK = 256
+SPLIT = 128
+
+
+def interleave(copy, dst, src):
+    copy(dst.rearrange("p (c i) j -> p c j i", i=4), src.rearrange("p j (c i) -> p c j i", i=4))
+
+
+def quantize(nc, codes, scales, grouped):
+    nc.vector.quantize_mx(out=codes.bitcast(FP8X4), scales=scales, in_=grouped)
+
+
+def tile_attend_refinescores_kernel(tc, query, fquery, ckeys, fkeys_words, fkeys_scales, fac, vals, offs, out):
+    nc = tc.nc
+    with ExitStack() as ctx:
+        sb = ctx.enter_context(tc.tile_pool(name="sb", bufs=1))
+        ps = ctx.enter_context(tc.psum_pool(name="ps", bufs=1))
+
+        def tile(name, shape, dtype, tag=""):
+            return sb.tile(shape, dtype, name=name, tag=tag or name, align_bytes=64)
+
+        def bank(name, shape, tag):
+            return ps.tile(shape, F32, name=name, tag=tag)
+
+        def act_copy(dst, src):
+            nc.scalar.activation(dst, src, ACT.Copy)
+
+        fk_scales = tile("fk_scales", [P, T], U8)
+        nc.vector.memset(fk_scales[:].bitcast(I32), 0)
+        offsets = tile("offsets", [P, I // 16], U16)
+        nc.sync.dma_start(offsets[:], offs)
+        q_raw = tile("q_raw", [P, PACK, Q], F32)
+        nc.sync.dma_start(q_raw[:], query.rearrange("(p j) q -> p j q", j=PACK))
+        fq_raw = tile("fq_raw", [P, 2, PACK * Q], F32)
+        nc.sync.dma_start(fq_raw[:], fquery.rearrange("(z p j) q -> p z (j q)", z=2, j=PACK))
+        fac_col = tile("fac_col", [P, 2, PACK], F32)
+        nc.sync.dma_start(fac_col[:], fac.rearrange("o (z p j) -> p (o z) j", z=2, j=PACK))
+        for quad in range(4):
+            nc.sync.dma_start(
+                fk_scales[32 * quad : 32 * quad + 8, :].bitcast(I32),
+                fkeys_scales[:, 4 * quad : 4 * quad + 4, :].bitcast(I32),
+            )
+        ck_view = ckeys.rearrange("(p j) t -> p j t", j=PACK)
+        ck_raw = []
+        for c in range(T // CHUNK):
+            raw = tile("ck_raw%d" % c, [P, PACK, CHUNK], F32)
+            nc.sync.dma_start(raw[:], ck_view[:, :, c * CHUNK : (c + 1) * CHUNK])
+            ck_raw.append(raw)
+        fk_words = []
+        for z in range(2):
+            words = tile("fk_words%d" % z, [P, T], I32)
+            nc.sync.dma_start(words[:], fkeys_words[z].rearrange("p n r -> p (n r)").bitcast(I32))
+            fk_words.append(words)
+        v_view = vals.rearrange("(z p j) e -> z p j e", z=2, j=PACK)
+        v_raw = []
+        for c in range(4):
+            z, h = divmod(c, 2)
+            raw = tile("v_raw%d" % c, [P, PACK, CHUNK], F32)
+            nc.sync.dma_start(raw[:], v_view[z][:, :, h * CHUNK : (h + 1) * CHUNK])
+            v_raw.append(raw)
+
+        ident = tile("ident", [P, P], F32)
+        make_identity(nc, ident[:])
+        df = tile("df", [P, T], F32)
+        nc.gpsimd.memset(df[:], 0.0)
+
+        q_bf = tile("q_bf", [P, Q, PACK], BF16)
+        interleave(nc.vector.tensor_copy, q_bf[:], q_raw[:])
+        q_codes = tile("q_codes", [P, Q], U32)
+        q_scales = tile("q_scales", [P, Q], U8)
+        quantize(nc, q_codes[:], q_scales[:], q_bf[:].rearrange("p c j -> p (c j)"))
+        fq_bf = tile("fq_bf", [P, 2, Q, PACK], BF16)
+        for z, copy in enumerate([act_copy, nc.vector.tensor_copy]):
+            interleave(copy, fq_bf[:, z], fq_raw[:, z, :].rearrange("p (j q) -> p j q", j=PACK))
+        fq_codes = tile("fq_codes", [P, 2 * Q], U32)
+        fq_scales = tile("fq_scales", [P, 2 * Q], U8)
+        quantize(nc, fq_codes[:], fq_scales[:], fq_bf[:].rearrange("p z c j -> p (z c j)"))
+        g_scales = tile("g_scales", [P, I], U8)
+        nc.vector.tensor_copy(g_scales[:], fk_scales[:].indirect(offsets[:]))
+
+        fac_ps = [bank("fac_ps%d" % z, [P, PACK, P], "fac%d" % z) for z in range(2)]
+        for z in range(2):
+            for j in range(PACK):
+                nc.tensor.transpose(fac_ps[z][:, j, :], fac_col[:, z, j : j + 1].to_broadcast([P, P]), ident[:])
+
+        a_sb = tile("a_sb", [P, T], F32)
+        for c in range(T // CHUNK):
+            ck_bf = tile("ck_bf%d" % c, [P, CHUNK, PACK], BF16)
+            interleave(nc.scalar.copy, ck_bf[:, :SPLIT, :], ck_raw[c][:, :, :SPLIT])
+            interleave(nc.vector.tensor_copy, ck_bf[:, SPLIT:, :], ck_raw[c][:, :, SPLIT:])
+            ck_codes = tile("ck_codes%d" % c, [P, CHUNK], U32)
+            ck_scales = tile("ck_scales%d" % c, [P, CHUNK], U8)
+            quantize(nc, ck_codes[:], ck_scales[:], ck_bf[:].rearrange("p c j -> p (c j)"))
+            a_ps = bank("a_ps%d" % c, [P, CHUNK], "ring%d" % c)
+            nc.tensor.matmul_mx(
+                out=a_ps[:],
+                lhsT=q_codes[:].bitcast(FP8X4),
+                lhsT_scale=q_scales[:],
+                rhs=ck_codes[:].bitcast(FP8X4),
+                rhs_scale=ck_scales[:],
+                start=True,
+                stop=True,
+            )
+            nc.scalar.copy(a_sb[:, c * CHUNK : (c + 1) * CHUNK], a_ps[:])
+
+        b_ps = bank("b_ps", [P, I], "b")
+        for z in range(2):
+            g_words = tile("g_words%d" % z, [P, I], U32)
+            nc.vector.tensor_copy(g_words[:], fk_words[z][:].bitcast(U32).indirect(offsets[:]))
+            nc.tensor.matmul_mx(
+                out=b_ps[:],
+                lhsT=fq_codes[:, z * Q : (z + 1) * Q].bitcast(FP8X4),
+                lhsT_scale=fq_scales[:, z * Q : (z + 1) * Q],
+                rhs=g_words[:].bitcast(FP8X4),
+                rhs_scale=g_scales[4 * z :, :],
+                start=(z == 0),
+                stop=(z == 1),
+            )
+        a_listed = tile("a_listed", [P, I], F32, tag="fk_words1")
+        nc.vector.tensor_copy(a_listed[:], a_sb[:].indirect(offsets[:]))
+        dl = tile("dl", [P, I], F32)
+        nc.vector.tensor_tensor(dl[:], b_ps[:], a_listed[:], ALU.subtract)
+        nc.vector.tensor_copy(df[:].indirect(offsets[:]), dl[:])
+
+        s = tile("s", [P, T], F32)
+        nc.vector.tensor_tensor(s[:], a_sb[:], df[:], ALU.add)
+        neg_s = tile("neg_s", [P, T], F32)
+        neg_max = tile("neg_max", [P, 1], F32)
+        nc.vector.tensor_scalar(neg_s[:], s[:], -1.0, None, ALU.mult, ALU.min, accum_out=neg_max[:])
+
+        v_bf0 = tile("v_bf0", [P, E, PACK], BF16)
+        v_bf2 = tile("v_bf2", [P, CHUNK, PACK], BF16)
+        interleave(nc.scalar.copy, v_bf0[:, :CHUNK, :], v_raw[0][:])
+        interleave(nc.scalar.copy, v_bf0[:, CHUNK:, :], v_raw[1][:])
+        interleave(nc.scalar.copy, v_bf2[:], v_raw[2][:])
+
+        prob = tile("prob", [P, T], F32, tag="v_raw2")
+        row_sum = tile("row_sum", [P, 1], F32)
+        nc.scalar.activation(prob[:], neg_s[:], ACT.Exp, bias=neg_max[:], scale=-1.0, accum_out=row_sum[:])
+        v_bf3 = tile("v_bf3", [P, CHUNK, PACK], BF16, tag="neg_s")
+        interleave(nc.scalar.copy, v_bf3[:], v_raw[3][:])
+
+        v_codes = tile("v_codes", [P, 2 * E], U32, tag="s")
+        v_scales = tile("v_scales", [P, 2 * E], U8)
+        quantize(nc, v_codes[:, :E], v_scales[:, :E], v_bf0[:].rearrange("p c j -> p (c j)"))
+        quantize(nc, v_codes[:, E : E + CHUNK], v_scales[:, E : E + CHUNK], v_bf2[:].rearrange("p c j -> p (c j)"))
+
+        inv_sum = tile("inv_sum", [P, 1], F32, tag="v_bf2")
+        nc.vector.reciprocal(inv_sum[:], row_sum[:])
+        wt_bf = [tile("wt_bf%d" % z, [P, Q, PACK], BF16) for z in range(2)]
+        for z in range(2):
+            wt_ps = bank("wt_ps%d" % z, [P, 2, Q], "ring%d" % z)
+            prob_z = prob[:, z * PASS : (z + 1) * PASS].rearrange("p (n j) -> p n j", j=PACK)
+            fac_z = fac_ps[z][:].rearrange("p j n -> p n j")
+            for u in range(2):
+                w = tile("w%d%d" % (z, u), [P, P, 2], BF16)
+                pair = slice(2 * u, 2 * u + 2)
+                nc.vector.scalar_tensor_tensor(w[:], prob_z[:, :, pair], inv_sum[:], fac_z[:, :, pair], ALU.mult, ALU.mult)
+                nc.tensor.transpose(wt_ps[:, u, :], w[:].rearrange("p n e -> p (n e)").bitcast(F32), ident[:])
+            nc.scalar.copy(
+                wt_bf[z][:].rearrange("p q j -> p (q j)").bitcast(F32).rearrange("p (q u) -> p q u", u=2),
+                wt_ps[:].rearrange("p u q -> p q u"),
+            )
+        wt_codes = [tile("wt_codes%d" % z, [P, Q], U32) for z in range(2)]
+        wt_scales = [tile("wt_scales%d" % z, [P, Q], U8) for z in range(2)]
+        o_ps = [bank("o_ps%d" % h, [P, CHUNK], "ring%d" % (2 + h)) for h in range(2)]
+        for z in range(2):
+            if z == 1:
+                quantize(nc, v_codes[:, E + CHUNK :], v_scales[:, E + CHUNK :], v_bf3[:].rearrange("p c j -> p (c j)"))
+            quantize(nc, wt_codes[z][:], wt_scales[z][:], wt_bf[z][:].rearrange("p q j -> p (q j)"))
+            for h in range(2):
+                cols = slice(z * E + h * CHUNK, z * E + (h + 1) * CHUNK)
+                nc.tensor.matmul_mx(
+                    out=o_ps[h][:],
+                    lhsT=wt_codes[z][:].bitcast(FP8X4),
+                    lhsT_scale=wt_scales[z][:],
+                    rhs=v_codes[:, cols].bitcast(FP8X4),
+                    rhs_scale=v_scales[:, cols],
+                    start=(z == 0),
+                    stop=(z == 1),
+                )
+        drains = [(nc.scalar.copy, nc.scalar), (nc.vector.tensor_copy, nc.sync)]
+        for h, (copy, queue) in enumerate(drains):
+            o_sb = tile("o_sb%d" % h, [P, CHUNK], F32)
+            copy(o_sb[:], o_ps[h][:])
+            queue.dma_start(out[:, h * CHUNK : (h + 1) * CHUNK], o_sb[:])

@@ -22,7 +22,7 @@ PACK = 4
 PASS = P * PACK
 BANK = 512
 CHUNK = 256
-SPLIT = 128
+SPLITS = (160, 128)
 
 
 def interleave(copy, dst, src):
@@ -50,25 +50,24 @@ def tile_attend_refinescores_kernel(tc, query, fquery, ckeys, fkeys_words, fkeys
 
         fk_scales = tile("fk_scales", [P, T], U8)
         nc.vector.memset(fk_scales[:].bitcast(I32), 0)
-        offsets = tile("offsets", [P, I // 16], U16)
-        nc.sync.dma_start(offsets[:], offs)
         q_raw = tile("q_raw", [P, PACK, Q], F32)
         nc.sync.dma_start(q_raw[:], query.rearrange("(p j) q -> p j q", j=PACK))
-        fq_raw = tile("fq_raw", [P, 2, PACK * Q], F32)
-        nc.sync.dma_start(fq_raw[:], fquery.rearrange("(z p j) q -> p z (j q)", z=2, j=PACK))
-        fac_col = tile("fac_col", [P, 2, PACK], F32)
-        nc.sync.dma_start(fac_col[:], fac.rearrange("o (z p j) -> p (o z) j", z=2, j=PACK))
-        for quad in range(4):
-            nc.sync.dma_start(
-                fk_scales[32 * quad : 32 * quad + 8, :].bitcast(I32),
-                fkeys_scales[:, 4 * quad : 4 * quad + 4, :].bitcast(I32),
-            )
+        offsets = tile("offsets", [P, I // 16], U16)
+        nc.sync.dma_start(offsets[:], offs)
         ck_view = ckeys.rearrange("(p j) t -> p j t", j=PACK)
         ck_raw = []
-        for c in range(T // CHUNK):
-            raw = tile("ck_raw%d" % c, [P, PACK, CHUNK], F32)
-            nc.sync.dma_start(raw[:], ck_view[:, :, c * CHUNK : (c + 1) * CHUNK])
+        for half in range(2):
+            raw = tile("ck_raw%d" % half, [P, PACK, BANK], F32)
+            nc.sync.dma_start(raw[:], ck_view[:, :, half * BANK : (half + 1) * BANK])
             ck_raw.append(raw)
+            if half == 0:
+                for quad in range(4):
+                    nc.sync.dma_start(
+                        fk_scales[32 * quad : 32 * quad + 8, :].bitcast(I32),
+                        fkeys_scales[:, 4 * quad : 4 * quad + 4, :].bitcast(I32),
+                    )
+        fq_raw = tile("fq_raw", [P, 2, PACK * Q], F32)
+        nc.sync.dma_start(fq_raw[:], fquery.rearrange("(z p j) q -> p z (j q)", z=2, j=PACK))
         fk_words = []
         for z in range(2):
             words = tile("fk_words%d" % z, [P, T], I32)
@@ -76,41 +75,35 @@ def tile_attend_refinescores_kernel(tc, query, fquery, ckeys, fkeys_words, fkeys
             fk_words.append(words)
         v_view = vals.rearrange("(z p j) e -> z p j e", z=2, j=PACK)
         v_raw = []
-        for c in range(4):
-            z, h = divmod(c, 2)
-            raw = tile("v_raw%d" % c, [P, PACK, CHUNK], F32)
-            nc.sync.dma_start(raw[:], v_view[z][:, :, h * CHUNK : (h + 1) * CHUNK])
+        for c, (z, first, width) in enumerate([(0, 0, E), (1, 0, CHUNK), (1, CHUNK, CHUNK)]):
+            raw = tile("v_raw%d" % c, [P, PACK, width], F32)
+            nc.sync.dma_start(raw[:], v_view[z][:, :, first : first + width])
             v_raw.append(raw)
+        fac_col = tile("fac_col", [P, 2, PACK], F32)
+        nc.sync.dma_start(fac_col[:], fac.rearrange("o (z p j) -> p (o z) j", z=2, j=PACK))
 
         ident = tile("ident", [P, P], F32)
         make_identity(nc, ident[:])
         df = tile("df", [P, T], F32)
         nc.gpsimd.memset(df[:], 0.0)
+        minus_one = tile("minus_one", [P, I], F32)
+        nc.vector.memset(minus_one[:], -1.0)
 
         q_bf = tile("q_bf", [P, Q, PACK], BF16)
         interleave(nc.vector.tensor_copy, q_bf[:], q_raw[:])
         q_codes = tile("q_codes", [P, Q], U32)
         q_scales = tile("q_scales", [P, Q], U8)
         quantize(nc, q_codes[:], q_scales[:], q_bf[:].rearrange("p c j -> p (c j)"))
-        fq_bf = tile("fq_bf", [P, 2, Q, PACK], BF16)
-        for z, copy in enumerate([act_copy, nc.vector.tensor_copy]):
-            interleave(copy, fq_bf[:, z], fq_raw[:, z, :].rearrange("p (j q) -> p j q", j=PACK))
-        fq_codes = tile("fq_codes", [P, 2 * Q], U32)
-        fq_scales = tile("fq_scales", [P, 2 * Q], U8)
-        quantize(nc, fq_codes[:], fq_scales[:], fq_bf[:].rearrange("p z c j -> p (z c j)"))
         g_scales = tile("g_scales", [P, I], U8)
         nc.vector.tensor_copy(g_scales[:], fk_scales[:].indirect(offsets[:]))
-
-        fac_ps = [bank("fac_ps%d" % z, [P, PACK, P], "fac%d" % z) for z in range(2)]
-        for z in range(2):
-            for j in range(PACK):
-                nc.tensor.transpose(fac_ps[z][:, j, :], fac_col[:, z, j : j + 1].to_broadcast([P, P]), ident[:])
 
         a_sb = tile("a_sb", [P, T], F32)
         for c in range(T // CHUNK):
             ck_bf = tile("ck_bf%d" % c, [P, CHUNK, PACK], BF16)
-            interleave(nc.scalar.copy, ck_bf[:, :SPLIT, :], ck_raw[c][:, :, :SPLIT])
-            interleave(nc.vector.tensor_copy, ck_bf[:, SPLIT:, :], ck_raw[c][:, :, SPLIT:])
+            first = (c % 2) * CHUNK
+            split = SPLITS[c // 2]
+            interleave(act_copy, ck_bf[:, :split, :], ck_raw[c // 2][:, :, first : first + split])
+            interleave(nc.vector.tensor_copy, ck_bf[:, split:, :], ck_raw[c // 2][:, :, first + split : first + CHUNK])
             ck_codes = tile("ck_codes%d" % c, [P, CHUNK], U32)
             ck_scales = tile("ck_scales%d" % c, [P, CHUNK], U8)
             quantize(nc, ck_codes[:], ck_scales[:], ck_bf[:].rearrange("p c j -> p (c j)"))
@@ -126,6 +119,12 @@ def tile_attend_refinescores_kernel(tc, query, fquery, ckeys, fkeys_words, fkeys
             )
             nc.scalar.copy(a_sb[:, c * CHUNK : (c + 1) * CHUNK], a_ps[:])
 
+        fq_bf = tile("fq_bf", [P, 2, Q, PACK], BF16)
+        for z, copy in enumerate([nc.scalar.copy, nc.vector.tensor_copy]):
+            interleave(copy, fq_bf[:, z], fq_raw[:, z, :].rearrange("p (j q) -> p j q", j=PACK))
+        fq_codes = tile("fq_codes", [P, 2 * Q], U32)
+        fq_scales = tile("fq_scales", [P, 2 * Q], U8)
+        quantize(nc, fq_codes[:], fq_scales[:], fq_bf[:].rearrange("p z c j -> p (z c j)"))
         b_ps = bank("b_ps", [P, I], "b")
         for z in range(2):
             g_words = tile("g_words%d" % z, [P, I], U32)
@@ -139,11 +138,11 @@ def tile_attend_refinescores_kernel(tc, query, fquery, ckeys, fkeys_words, fkeys
                 start=(z == 0),
                 stop=(z == 1),
             )
-        a_listed = tile("a_listed", [P, I], F32, tag="fk_words1")
-        nc.vector.tensor_copy(a_listed[:], a_sb[:].indirect(offsets[:]))
-        dl = tile("dl", [P, I], F32)
-        nc.vector.tensor_tensor(dl[:], b_ps[:], a_listed[:], ALU.subtract)
-        nc.vector.tensor_copy(df[:].indirect(offsets[:]), dl[:])
+        neg_a_listed = tile("neg_a_listed", [P, I], F32, tag="fk_words1")
+        nc.vector.tensor_tensor(neg_a_listed[:], a_sb[:].indirect(offsets[:]), minus_one[:], ALU.mult)
+        b_sb = tile("b_sb", [P, I], F32)
+        nc.scalar.copy(b_sb[:], b_ps[:])
+        nc.vector.tensor_tensor(df[:].indirect(offsets[:]), b_sb[:], neg_a_listed[:], ALU.add)
 
         s = tile("s", [P, T], F32)
         nc.vector.tensor_tensor(s[:], a_sb[:], df[:], ALU.add)
@@ -152,23 +151,26 @@ def tile_attend_refinescores_kernel(tc, query, fquery, ckeys, fkeys_words, fkeys
         nc.vector.tensor_scalar(neg_s[:], s[:], -1.0, None, ALU.mult, ALU.min, accum_out=neg_max[:])
 
         v_bf0 = tile("v_bf0", [P, E, PACK], BF16)
-        v_bf2 = tile("v_bf2", [P, CHUNK, PACK], BF16)
-        interleave(nc.scalar.copy, v_bf0[:, :CHUNK, :], v_raw[0][:])
-        interleave(nc.scalar.copy, v_bf0[:, CHUNK:, :], v_raw[1][:])
-        interleave(nc.scalar.copy, v_bf2[:], v_raw[2][:])
+        interleave(nc.scalar.copy, v_bf0[:], v_raw[0][:])
 
-        prob = tile("prob", [P, T], F32, tag="v_raw2")
+        prob = tile("prob", [P, T], F32, tag="v_raw0")
         row_sum = tile("row_sum", [P, 1], F32)
         nc.scalar.activation(prob[:], neg_s[:], ACT.Exp, bias=neg_max[:], scale=-1.0, accum_out=row_sum[:])
         v_bf3 = tile("v_bf3", [P, CHUNK, PACK], BF16, tag="neg_s")
-        interleave(nc.scalar.copy, v_bf3[:], v_raw[3][:])
+        interleave(nc.scalar.copy, v_bf3[:], v_raw[2][:])
 
         v_codes = tile("v_codes", [P, 2 * E], U32, tag="s")
         v_scales = tile("v_scales", [P, 2 * E], U8)
         quantize(nc, v_codes[:, :E], v_scales[:, :E], v_bf0[:].rearrange("p c j -> p (c j)"))
-        quantize(nc, v_codes[:, E : E + CHUNK], v_scales[:, E : E + CHUNK], v_bf2[:].rearrange("p c j -> p (c j)"))
+        v_bf2 = tile("v_bf2", [P, CHUNK, PACK], BF16, tag="v_bf0")
+        interleave(nc.vector.tensor_copy, v_bf2[:], v_raw[1][:])
 
-        inv_sum = tile("inv_sum", [P, 1], F32, tag="v_bf2")
+        fac_ps = [bank("fac_ps%d" % z, [P, PACK, P], "fac%d" % z) for z in range(2)]
+        for z in range(2):
+            for j in range(PACK):
+                nc.tensor.transpose(fac_ps[z][:, j, :], fac_col[:, z, j : j + 1].to_broadcast([P, P]), ident[:])
+
+        inv_sum = tile("inv_sum", [P, 1], F32, tag="v_raw1")
         nc.vector.reciprocal(inv_sum[:], row_sum[:])
         wt_bf = [tile("wt_bf%d" % z, [P, Q, PACK], BF16) for z in range(2)]
         for z in range(2):
@@ -189,6 +191,7 @@ def tile_attend_refinescores_kernel(tc, query, fquery, ckeys, fkeys_words, fkeys
         o_ps = [bank("o_ps%d" % h, [P, CHUNK], "ring%d" % (2 + h)) for h in range(2)]
         for z in range(2):
             if z == 1:
+                quantize(nc, v_codes[:, E : E + CHUNK], v_scales[:, E : E + CHUNK], v_bf2[:].rearrange("p c j -> p (c j)"))
                 quantize(nc, v_codes[:, E + CHUNK :], v_scales[:, E + CHUNK :], v_bf3[:].rearrange("p c j -> p (c j)"))
             quantize(nc, wt_codes[z][:], wt_scales[z][:], wt_bf[z][:].rearrange("p q j -> p (q j)"))
             for h in range(2):

from contextlib import ExitStack

import concourse.mybir as mybir
from concourse.masks import make_identity

D, K, T, I, Q, E = 512, 1024, 1024, 256, 128, 512
FLOPS = 2 * Q * (D * T + K * I + T * E)

F32 = mybir.dt.float32
BF16 = mybir.dt.bfloat16
I32 = mybir.dt.int32
U32 = mybir.dt.uint32
U16 = mybir.dt.uint16
U8 = mybir.dt.uint8
FP8X4 = mybir.dt.float8_e4m3fn_x4
ALU = mybir.AluOpType
ACT = mybir.ActivationFunctionType
AX = mybir.AxisListType

P = 128
PACK = 4
PASS = P * PACK
BANK = 512
CHUNK = 256
SPLITS = (160, 128)


def interleave(copy, dst, src):
    copy(dst.rearrange("p (c i) j -> p c j i", i=4), src.rearrange("p j (c i) -> p c j i", i=4))


def quantize(nc, codes, scales, grouped):
    nc.vector.quantize_mx(out=codes.bitcast(FP8X4), scales=scales, in_=grouped)


def tile_attend_refinescores_kernel(tc, query, fquery, ckeys, fkeys_words, fkeys_scales, fac, vals, offs, out):
    nc = tc.nc
    with ExitStack() as ctx:
        sb = ctx.enter_context(tc.tile_pool(name="sb", bufs=1))
        ps = ctx.enter_context(tc.psum_pool(name="ps", bufs=1))

        def tile(name, shape, dtype, tag=""):
            return sb.tile(shape, dtype, name=name, tag=tag or name, align_bytes=64)

        def bank(name, shape, tag):
            return ps.tile(shape, F32, name=name, tag=tag)

        def act_copy(dst, src):
            nc.scalar.activation(dst, src, ACT.Copy)

        fk_scales = tile("fk_scales", [P, T], U8)
        nc.vector.memset(fk_scales[:].bitcast(I32), 0)
        q_raw = tile("q_raw", [P, PACK, Q], F32)
        nc.sync.dma_start(q_raw[:], query.rearrange("(p j) q -> p j q", j=PACK))
        offsets = tile("offsets", [P, I // 16], U16)
        nc.sync.dma_start(offsets[:], offs)
        ck_view = ckeys.rearrange("(p j) t -> p j t", j=PACK)
        ck_raw = []
        for half in range(2):
            raw = tile("ck_raw%d" % half, [P, PACK, BANK], F32)
            nc.sync.dma_start(raw[:], ck_view[:, :, half * BANK : (half + 1) * BANK])
            ck_raw.append(raw)
            if half == 0:
                for quad in range(4):
                    nc.sync.dma_start(
                        fk_scales[32 * quad : 32 * quad + 8, :].bitcast(I32),
                        fkeys_scales[:, 4 * quad : 4 * quad + 4, :].bitcast(I32),
                    )
        fq_raw = tile("fq_raw", [P, 2, PACK * Q], F32)
        nc.sync.dma_start(fq_raw[:], fquery.rearrange("(z p j) q -> p z (j q)", z=2, j=PACK))
        fk_words = []
        for z in range(2):
            words = tile("fk_words%d" % z, [P, T], I32)
            nc.sync.dma_start(words[:], fkeys_words[z].rearrange("p n r -> p (n r)").bitcast(I32))
            fk_words.append(words)
        v_view = vals.rearrange("(z p j) e -> z p j e", z=2, j=PACK)
        v_raw = []
        for c, (z, first, width) in enumerate([(0, 0, E), (1, 0, CHUNK), (1, CHUNK, CHUNK)]):
            raw = tile("v_raw%d" % c, [P, PACK, width], F32)
            nc.sync.dma_start(raw[:], v_view[z][:, :, first : first + width])
            v_raw.append(raw)
        fac_col = tile("fac_col", [P, 2, PACK], F32)
        nc.sync.dma_start(fac_col[:], fac.rearrange("o (z p j) -> p (o z) j", z=2, j=PACK))

        ident = tile("ident", [P, P], F32)
        make_identity(nc, ident[:])
        df = tile("df", [P, T], F32)
        nc.gpsimd.memset(df[:], 0.0)
        minus_one = tile("minus_one", [P, I], F32)
        nc.vector.memset(minus_one[:], -1.0)

        q_bf = tile("q_bf", [P, Q, PACK], BF16)
        interleave(nc.vector.tensor_copy, q_bf[:], q_raw[:])
        q_codes = tile("q_codes", [P, Q], U32)
        q_scales = tile("q_scales", [P, Q], U8)
        quantize(nc, q_codes[:], q_scales[:], q_bf[:].rearrange("p c j -> p (c j)"))
        g_scales = tile("g_scales", [P, I], U8)
        nc.vector.tensor_copy(g_scales[:], fk_scales[:].indirect(offsets[:]))

        a_sb = tile("a_sb", [P, T], F32)
        for c in range(T // CHUNK):
            ck_bf = tile("ck_bf%d" % c, [P, CHUNK, PACK], BF16)
            first = (c % 2) * CHUNK
            split = SPLITS[c // 2]
            interleave(act_copy, ck_bf[:, :split, :], ck_raw[c // 2][:, :, first : first + split])
            interleave(nc.vector.tensor_copy, ck_bf[:, split:, :], ck_raw[c // 2][:, :, first + split : first + CHUNK])
            ck_codes = tile("ck_codes%d" % c, [P, CHUNK], U32)
            ck_scales = tile("ck_scales%d" % c, [P, CHUNK], U8)
            quantize(nc, ck_codes[:], ck_scales[:], ck_bf[:].rearrange("p c j -> p (c j)"))
            a_ps = bank("a_ps%d" % c, [P, CHUNK], "ring%d" % c)
            nc.tensor.matmul_mx(
                out=a_ps[:],
                lhsT=q_codes[:].bitcast(FP8X4),
                lhsT_scale=q_scales[:],
                rhs=ck_codes[:].bitcast(FP8X4),
                rhs_scale=ck_scales[:],
                start=True,
                stop=True,
            )
            nc.scalar.copy(a_sb[:, c * CHUNK : (c + 1) * CHUNK], a_ps[:])

        fq_bf = tile("fq_bf", [P, 2, Q, PACK], BF16)
        for z, copy in enumerate([nc.scalar.copy, nc.vector.tensor_copy]):
            interleave(copy, fq_bf[:, z], fq_raw[:, z, :].rearrange("p (j q) -> p j q", j=PACK))
        fq_codes = tile("fq_codes", [P, 2 * Q], U32)
        fq_scales = tile("fq_scales", [P, 2 * Q], U8)
        quantize(nc, fq_codes[:], fq_scales[:], fq_bf[:].rearrange("p z c j -> p (z c j)"))
        b_ps = bank("b_ps", [P, I], "b")
        for z in range(2):
            g_words = tile("g_words%d" % z, [P, I], U32)
            nc.vector.tensor_copy(g_words[:], fk_words[z][:].bitcast(U32).indirect(offsets[:]))
            nc.tensor.matmul_mx(
                out=b_ps[:],
                lhsT=fq_codes[:, z * Q : (z + 1) * Q].bitcast(FP8X4),
                lhsT_scale=fq_scales[:, z * Q : (z + 1) * Q],
                rhs=g_words[:].bitcast(FP8X4),
                rhs_scale=g_scales[4 * z :, :],
                start=(z == 0),
                stop=(z == 1),
            )
        neg_a_listed = tile("neg_a_listed", [P, I], F32, tag="fk_words1")
        nc.vector.tensor_tensor(neg_a_listed[:], a_sb[:].indirect(offsets[:]), minus_one[:], ALU.mult)
        b_sb = tile("b_sb", [P, I], F32)
        nc.scalar.copy(b_sb[:], b_ps[:])
        nc.vector.tensor_tensor(df[:].indirect(offsets[:]), b_sb[:], neg_a_listed[:], ALU.add)

        s = tile("s", [P, T], F32)
        nc.vector.tensor_tensor(s[:], a_sb[:], df[:], ALU.add)
        neg_s = tile("neg_s", [P, T], F32)
        neg_max = tile("neg_max", [P, 1], F32)
        nc.vector.tensor_scalar(neg_s[:], s[:], -1.0, None, ALU.mult, ALU.min, accum_out=neg_max[:])

        v_bf0 = tile("v_bf0", [P, E, PACK], BF16)
        interleave(nc.scalar.copy, v_bf0[:], v_raw[0][:])

        prob = tile("prob", [P, T], F32, tag="v_raw0")
        row_sum = tile("row_sum", [P, 1], F32)
        nc.scalar.activation(prob[:], neg_s[:], ACT.Exp, bias=neg_max[:], scale=-1.0, accum_out=row_sum[:])
        v_bf3 = tile("v_bf3", [P, CHUNK, PACK], BF16, tag="neg_s")
        interleave(nc.scalar.copy, v_bf3[:], v_raw[2][:])

        v_codes = tile("v_codes", [P, 2 * E], U32, tag="s")
        v_scales = tile("v_scales", [P, 2 * E], U8)
        quantize(nc, v_codes[:, :E], v_scales[:, :E], v_bf0[:].rearrange("p c j -> p (c j)"))
        v_bf2 = tile("v_bf2", [P, CHUNK, PACK], BF16, tag="v_bf0")
        interleave(nc.vector.tensor_copy, v_bf2[:], v_raw[1][:])

        fac_ps = [bank("fac_ps%d" % z, [P, PACK, P], "fac%d" % z) for z in range(2)]
        for z in range(2):
            for j in range(PACK):
                nc.tensor.transpose(fac_ps[z][:, j, :], fac_col[:, z, j : j + 1].to_broadcast([P, P]), ident[:])

        inv_sum = tile("inv_sum", [P, 1], F32, tag="v_raw1")
        nc.vector.reciprocal(inv_sum[:], row_sum[:])
        wt_bf = [tile("wt_bf%d" % z, [P, Q, PACK], BF16) for z in range(2)]
        for z in range(2):
            wt_ps = bank("wt_ps%d" % z, [P, 2, Q], "ring%d" % z)
            prob_z = prob[:, z * PASS : (z + 1) * PASS].rearrange("p (n j) -> p n j", j=PACK)
            fac_z = fac_ps[z][:].rearrange("p j n -> p n j")
            for u in range(2):
                w = tile("w%d%d" % (z, u), [P, P, 2], BF16)
                pair = slice(2 * u, 2 * u + 2)
                nc.vector.scalar_tensor_tensor(w[:], prob_z[:, :, pair], inv_sum[:], fac_z[:, :, pair], ALU.mult, ALU.mult)
                nc.tensor.transpose(wt_ps[:, u, :], w[:].rearrange("p n e -> p (n e)").bitcast(F32), ident[:])
            nc.scalar.copy(
                wt_bf[z][:].rearrange("p q j -> p (q j)").bitcast(F32).rearrange("p (q u) -> p q u", u=2),
                wt_ps[:].rearrange("p u q -> p q u"),
            )
        wt_codes = [tile("wt_codes%d" % z, [P, Q], U32) for z in range(2)]
        wt_scales = [tile("wt_scales%d" % z, [P, Q], U8) for z in range(2)]
        o_ps = [bank("o_ps%d" % h, [P, CHUNK], "ring%d" % (2 + h)) for h in range(2)]
        for z in range(2):
            if z == 1:
                quantize(nc, v_codes[:, E : E + CHUNK], v_scales[:, E : E + CHUNK], v_bf2[:].rearrange("p c j -> p (c j)"))
                quantize(nc, v_codes[:, E + CHUNK :], v_scales[:, E + CHUNK :], v_bf3[:].rearrange("p c j -> p (c j)"))
            quantize(nc, wt_codes[z][:], wt_scales[z][:], wt_bf[z][:].rearrange("p q j -> p (q j)"))
            for h in range(2):
                cols = slice(z * E + h * CHUNK, z * E + (h + 1) * CHUNK)
                nc.tensor.matmul_mx(
                    out=o_ps[h][:],
                    lhsT=wt_codes[z][:].bitcast(FP8X4),
                    lhsT_scale=wt_scales[z][:],
                    rhs=v_codes[:, cols].bitcast(FP8X4),
                    rhs_scale=v_scales[:, cols],
                    start=(z == 0),
                    stop=(z == 1),
                )
        drains = [(nc.scalar.copy, nc.scalar), (nc.vector.tensor_copy, nc.sync)]
        for h, (copy, queue) in enumerate(drains):
            o_sb = tile("o_sb%d" % h, [P, CHUNK], F32)
            copy(o_sb[:], o_ps[h][:])
            queue.dma_start(out[:, h * CHUNK : (h + 1) * CHUNK], o_sb[:])
